import numpy as np, ml_dtypes
CORES = [35,38,43,46]
N = 4
BF = ml_dtypes.bfloat16
def gentries(a):
    return np.ascontiguousarray(a.reshape(8, 16, -1).transpose(0, 2, 1)).reshape(8, -1)
def gtable(e):
    e = np.asarray(e); return np.ascontiguousarray(e.reshape(8, -1, 16).transpose(0, 2, 1)).reshape(128, -1).astype(np.int32)
W, C, RO = 4096, 256, 4
LA, LB, LE, WD = 864, 1024, 1024, 32
def parts(rng):
    x = rng.integers(0, 256, (N, 8, 16, W)); a = rng.integers(0, W, (N, 8, C, 16)); p = rng.integers(0, W, (N, 8, C, 16))
    pool = rng.integers(0, W, (N, 8, 32)); hot = np.take_along_axis(pool, rng.integers(0, 32, (N, 8, C * 16)), 2).reshape(N, 8, C, 16)
    return x, a, np.where(rng.random((N, 8, C, 16)) < 0.3, hot, p)
def pack(x, a, p):
    return {"x0": np.ascontiguousarray(x.reshape(N, 128, W)).astype(np.float32).astype(BF), "ka": np.stack([gtable(v.reshape(8, -1)) for v in a]), "ph": np.stack([gtable(v.reshape(8, -1)) for v in p])}
def alike(rng, a, p, share):
    m = (rng.random((N, 8, C, 1)) < share) & (np.arange(16) == rng.integers(0, 16, (N, 8, C, 1)))
    return np.where(m, a, p)
def setup_inputs(rng):
    x, a, p = parts(rng)
    return pack(x, a, alike(rng, a, p, 0.08))
def setup_inputs_spread(rng):
    x, a, p = parts(rng)
    v = np.minimum((np.exp2(8 * rng.random((N, 8, 1, W))) * rng.random(x.shape)).astype(np.int64), 255)
    x = np.where(rng.random(x.shape) < 0.5, v, 255 - v)
    a = np.minimum((W * rng.random(a.shape) ** 2).astype(np.int64), W - 1); u = np.minimum((W * rng.random(a.shape) ** 3).astype(np.int64), W - 1)
    return pack(x, a, np.where(rng.random(a.shape) < 0.5, u, p))
def setup_inputs_ends(rng):
    x, a, p = parts(rng); x = 255 * rng.integers(0, 2, x.shape)
    h = rng.choice(np.array([3, 4, 4, 5, 16]), (N, 8)); h[N - 1, 7] = 16; h[0, 7] = 4; h[0, 0] = 4; h[0, 1] = 3; h[N - 1, 6] = 4
    for r in range(N):
        for g in range(8):
            w = x[r, g]; w[:, W - 1] = w[:, 0]; o = rng.permutation(16)[:h[r, g]]
            if h[r, g] == 16: w[:, 0] = 0
            w[o, W - 1] = 255 - w[o, 0]
    kind = rng.choice(np.array([0, 1, 2]), (N, 8, C, 1), p=[0.4, 0.34, 0.26]); kind[:, :, [0, 1, 3, C - 2, C - 1]] = 0
    e = rng.integers(0, 2, (N, 8, C, 1))
    a = np.where(kind == 0, e * (W - 1), np.where(kind == 1, (W - 1) * rng.integers(0, 2, a.shape), a))
    p = np.where(kind == 0, (1 - e) * (W - 1), np.where(kind == 1, (W - 1) * rng.integers(0, 2, a.shape), p))
    return pack(x, a, p)
def setup_inputs_corners(rng):
    x = np.zeros((N, 8, 16, W), np.int64); a = np.zeros((N, 8, C, 16), np.int64); p = np.zeros((N, 8, C, 16), np.int64)
    far = np.array([LA - 1, LA, LA + 1, LB - 1, LB, LB + 3, LB + 4, LB + 59, LB + 60]); h = W // 2; M = 36; lane = np.arange(16)
    signs = np.stack([np.ones(16, np.int64), -np.ones(16, np.int64), 1 - 2 * (lane & 1)])
    for g in range(8):
        q = rng.permutation(W); low = q[1:h]; high = q[h + M:]; mids = q[h:h + M]
        m0 = rng.choice(np.array([-1, 0, 15, 15, 6]), C); o = lane[None, :] == m0[:, None]; o = o ^ (rng.random((C, 1)) < 0.5)
        k = rng.integers(0, 16, C); k = np.where(k == m0, (k + 1) & 15, k); swap = rng.random(C) < 0.5
        for r in range(N):
            w = x[r, g]; w[:, low] = rng.integers(0, 31, (16, len(low))); w[:, high] = rng.integers(215, 256, (16, len(high)))
            b = rng.integers(100, 151, 16); w[:, q[0]] = b; T = rng.permutation(np.resize(far, M))
            am = T[None, :] // 16 + (lane[:, None] < T[None, :] % 16); w[:, mids] = b[:, None] + am * signs[rng.integers(0, 3, M)].T
            lo1 = low[rng.integers(0, len(low), (C, 16))]; lo2 = low[rng.integers(0, len(low), (C, 16))]; hi1 = high[rng.integers(0, len(high), (C, 16))]; hi2 = high[rng.integers(0, len(high), (C, 16))]
            u = np.where(o, hi1, lo1); v = np.where(o, lo2, hi2)
            n = (0, 16, 15, C, 1, 17, 14, 31)[(g + 3 * r) % 8]; oc = rng.permutation(C); die = oc[:n]; rest = oc[n:]
            v[die, k[die]] = np.where(o[die, k[die]], hi2[die, k[die]], lo2[die, k[die]])
            edge = die[1::2]; under = mids[T == LA - 1]; md = under[rng.integers(0, len(under), len(edge))]
            u[edge, k[edge]] = np.where(swap[edge], md, q[0]); v[edge, k[edge]] = np.where(swap[edge], q[0], md)
            over = mids[T >= LA]; md = over[rng.integers(0, len(over), len(rest))]
            u[rest, k[rest]] = np.where(swap[rest], md, q[0]); v[rest, k[rest]] = np.where(swap[rest], q[0], md)
            assert int(np.sum(np.min(np.add.reduce(np.abs(w[:, u] - w[:, v]), axis=0), axis=1) < LA)) == n
            a[r, g] = u; p[r, g] = v
    return pack(x, a, p)
def setup_inputs_full(rng):
    x, a, p = parts(rng); lane = np.arange(16); h = W // 2; u = W // 4; z = int(rng.integers(0, N)); dead = int(rng.integers(0, 8))
    for g in range(8):
        if g == dead: continue
        for r in range(N):
            w = x[r, g]; q = rng.permutation(W); right = q[:h]; left = q[h:h + u]; out = q[h + u:]; b = rng.integers(100, 151, (16, 1))
            w[:, right] = b + rng.integers(0, 4, (16, h))
            far = np.where(rng.random((16, u)) < 0.5, 78 + rng.integers(0, 3, (16, u)), -75 - rng.integers(0, 3, (16, u)))
            near = np.argsort(rng.random((16, u)), axis=0) < 4
            w[:, left] = b + np.where(near, rng.integers(-8, 12, (16, u)), far)
            w[:, out] = b + rng.integers(90, 100, (16, len(out))) * (1 - 2 * rng.integers(0, 2, (16, len(out))))
            i = (rng.permutation(h)[:C], np.full(C, int(rng.integers(0, h))), rng.integers(0, 6, C))[(g + r) % 3]
            here = lane[None, :] == rng.integers(0, 16, (C, 1))
            a[r, g] = np.where(here, left[rng.integers(0, u, (C, 16))], right[rng.integers(0, h, (C, 16))])
            p[r, g] = np.where(here, right[i][:, None], out[rng.integers(0, len(out), (C, 16))])
    q = rng.permutation(np.arange(1, W)); s1 = q[:h]; s2 = q[h:h + u]; s0 = np.append(q[h + u:], 0)
    a[:, dead] = 0; p[:, dead] = s0[rng.integers(0, len(s0), (N, C, 16))]
    far = np.array([LB - 1, LB, LB + 1, LB + 3, LB + 4, LB + 31, LB + 59, LB + 60]); T = far[np.arange(h) % 8]
    cl = np.minimum(rng.integers(0, 8, (C, 1)) + rng.integers(0, 3, (C, 16)), 7)
    a[(z - 2) % N, dead] = s1[cl + 8 * rng.integers(0, h // 8, (C, 16))]; p[(z + 2) % N, dead] = s2[rng.integers(0, u, (C, 16))]
    x[:, dead] = rng.integers(215, 256, (N, 16, W))
    for r in range(N):
        w = x[r, dead]; w[:, s1] = rng.integers(0, 31, (16, h))
        if r == z:
            b = rng.integers(100, 151, (16, 1)); w[:] = b + rng.integers(0, 4, (16, W)); w[:, s2] = b
            w[:, s1] = b + (T[None, :] // 16 + (lane[:, None] < T[None, :] % 16)) * (1 - 2 * rng.integers(0, 2, (16, h)))
    return pack(x, a, p)
def setup_inputs_ties(rng):
    x, a, p = parts(rng); x = rng.integers(0, 176, x.shape)
    pool = rng.integers(0, W, (N, 8, 8)); pool[..., 0] = 0; pool[..., 7] = W - 1
    hot = np.take_along_axis(pool, rng.integers(0, 8, (N, 8, C * 16)), 2).reshape(N, 8, C, 16); p[:, 1::2] = hot[:, 1::2]
    src = np.arange(16) % rng.choice(np.array([1, 1, 1, 2, 4, 16]), (N, 8, C, 1))
    return pack(x, np.take_along_axis(a, src, 3), np.take_along_axis(p, src, 3))
def check_inputs(d):
    bad = []
    for k, lo, hi in (("x0", 0, 255), ("ka", 0, W - 1), ("ph", 0, W - 1)):
        v = np.asarray(d[k]).astype(np.float64)
        if not (np.min(v) >= lo and np.max(v) <= hi): bad.append("range of " + k)
    v = np.asarray(d["x0"]).astype(np.float64)
    if np.any(v != np.floor(v)): bad.append("whole numbers of x0")
    return bad
def reference(x0, ka, ph):
    X = x0.astype(np.float32).astype(np.int32).reshape(N, 8, 16, W)
    K = np.stack([gentries(v) for v in ka]).astype(np.int64).reshape(N, 8, C, 16)
    P = np.stack([gentries(v) for v in ph]).astype(np.int64).reshape(N, 8, C, 16)
    A = np.zeros((N, 8, 1), np.int64); place = np.arange(16)
    for t in range(RO):
        if t > 0: K = np.roll(K, 1, axis=0); P = np.roll(P, -1, axis=0)
        for r in range(N):
            x, a, p = X[r], K[r].copy(), P[r].copy()
            s = np.take_along_axis(x, a.reshape(8, 1, C * 16), 2).reshape(8, 16, C, 16); y = np.take_along_axis(x, p.reshape(8, 1, C * 16), 2).reshape(8, 16, C, 16)
            D = np.add.reduce(np.abs(s - y), axis=1)
            k = np.argmin(D, axis=2)
            d = np.take_along_axis(D, k[:, :, None], 2)[:, :, 0]
            sk = np.take_along_axis(s, k[:, None, :, None], 3)[..., 0]; yk = np.take_along_axis(y, k[:, None, :, None], 3)[..., 0]
            kill = d < LA; prime = ~kill & (d < LB + 4 * (A[r] & 15))
            step = np.where(np.add.reduce(sk, axis=1) > np.add.reduce(yk, axis=1), 1, -1) * (1 + (d & 3))
            n = np.take_along_axis(p, ((k + step) & 15)[:, :, None], 2)[:, :, 0]
            xn = np.take_along_axis(x, n[:, None, :], 2)
            near = np.add.reduce(np.abs(s - xn[..., None]), axis=1) < LE
            m = np.where(np.any(near, axis=2), np.argmax(near, axis=2), -1)
            fresh = np.take_along_axis(a, np.clip(m[:, :, None] + place, 0, 15), 2); fresh[:, :, 0] = n
            v = np.take_along_axis(p, k[:, :, None], 2)[:, :, 0]; new = np.where(np.abs(sk - yk) <= WD, (yk + 128) & 255, yk)
            for g in range(8):
                c = np.nonzero(prime[g])[0]; w = c[np.unique(v[g, c], return_index=True)[1]]
                x[g][:, v[g, w]] = new[g][:, w]
            P[r] = np.where(kill[:, :, None], (((a * p) >> 5) + p) & (W - 1), p)
            K[r] = np.where(prime[:, :, None], fresh, a)
            A[r] = A[r] + np.add.reduce(kill.astype(np.int64), axis=1)[:, None]
    return {"yk": np.stack([gtable(v.reshape(8, -1)) for v in K]).astype(np.float32), "yp": np.stack([gtable(v.reshape(8, -1)) for v in P]).astype(np.float32), "yx": X.reshape(N, 128, W).astype(np.float32).astype(BF)}

import numpy as np
from concourse.mybir import AluOpType as A, ActivationFunctionType as F

R, H, LO = 4, 128, 16
NB1 = 0
CH = 4
BIG = float(2 ** 30)
OFF = 65536.0
FW, WW, XW = 18 * 256, 18 * 256, 4352

SCRATCH = {
    "X": ("sbuf", [128, XW], "bfloat16"),
    "KI": ("sbuf", [128, 256], "int32"), "PI": ("sbuf", [128, 256], "int32"),
    "KF": ("sbuf", [128, 256], "float32"), "PF": ("sbuf", [128, 256], "float32"),
    "Y0": ("sbuf", [128, 2048], "bfloat16"), "D0": ("sbuf", [128, 2048], "bfloat16"), "R0": ("sbuf", [128, 2048], "bfloat16"),
    "S1": ("sbuf", [128, 2048], "bfloat16"), "D1": ("sbuf", [128, 2048], "bfloat16"), "R1": ("sbuf", [128, 2048], "bfloat16"),
    "A0": ("sbuf", [128, 2048], "bfloat16"), "A1": ("sbuf", [128, 2048], "bfloat16"), "M1": ("sbuf", [128, 2048], "bfloat16"),
    "KM": ("sbuf", [128, 256], "float32"), "KC": ("sbuf", [128, 256], "float32"), "QM": ("sbuf", [128, 256], "float32"),
    "KB": ("sbuf", [128, 256], "bfloat16"),
    "LI": ("sbuf", [128, 256], "int32"), "LF": ("sbuf", [128, 336], "float32"),
    "uf0": ("sbuf", [128, 8], "uint16"), "uf1": ("sbuf", [128, 8], "uint16"), "uk": ("sbuf", [128, 16], "uint16"),
    "uu": ("sbuf", [128, 16], "uint16"), "uWV": ("sbuf", [128, 32], "uint16"), "uX": ("sbuf", [128, 16], "uint16"),
    "XN0": ("sbuf", [128, 128], "bfloat16"), "XN1": ("sbuf", [128, 128], "bfloat16"), "SF1": ("sbuf", [128, 128], "bfloat16"),
    "SK1": ("sbuf", [128, 128], "bfloat16"), "YK": ("sbuf", [128, 256], "bfloat16"), "AD": ("sbuf", [128, 256], "bfloat16"),
    "w2": ("sbuf", [128, 256], "bfloat16"), "wg": ("sbuf", [128, 256], "bfloat16"),
    "pen": ("sbuf", [128, 256], "bfloat16"), "ts": ("sbuf", [128, 256], "bfloat16"), "tb": ("sbuf", [128, 256], "bfloat16"), "tm": ("sbuf", [128, 256], "bfloat16"),
    "kp": ("sbuf", [128, 256], "int32"), "kq": ("sbuf", [128, 256], "int32"), "p1": ("sbuf", [128, 256], "int32"), "p2": ("sbuf", [128, 256], "int32"), "p3": ("sbuf", [128, 256], "int32"),
    "KD": ("sbuf", [128, 256], "float32"), "K15": ("sbuf", [128, 256], "float32"), "BA": ("sbuf", [128, 256], "float32"), "KN": ("sbuf", [128, 256], "float32"),
    "W": ("sbuf", [128, WW], "float32"), "FF": ("sbuf", [128, FW], "float32"), "kd": ("dram", [8, 17, 256], "float32"),
    "VG": ("sbuf", [128, 256], "float32"), "RU": ("sbuf", [128, 256], "float32"), "Vu": ("sbuf", [128, 256], "uint16"),
    "FD": ("sbuf", [128, 256], "bfloat16"), "EQ": ("sbuf", [128, 15 * 256], "bfloat16"), "SE": ("sbuf", [128, 256], "float32"),
    "KJ": ("sbuf", [128, 256], "bfloat16"),
    "ia": ("sbuf", [128, 256], "int32"), "ib": ("sbuf", [128, 256], "int32"), "ic": ("sbuf", [128, 256], "int32"), "idd": ("sbuf", [128, 256], "int32"),
    "If": ("sbuf", [128, 128], "float32"), "Ib": ("sbuf", [128, 128], "bfloat16"), "In": ("sbuf", [128, 128], "bfloat16"),
    "mf": ("sbuf", [128, 128], "float32"), "mb": ("sbuf", [128, 128], "bfloat16"), "OD": ("sbuf", [128, 256], "bfloat16"),
    "B8f": ("sbuf", [128, 8], "float32"), "B8": ("sbuf", [128, 8], "bfloat16"), "B8n": ("sbuf", [128, 8], "bfloat16"), "B82": ("sbuf", [128, 8], "bfloat16"),
    "WN": ("sbuf", [128, 8], "bfloat16"), "WR": ("sbuf", [128, 8], "bfloat16"), "WP": ("sbuf", [128, 8], "bfloat16"),
    "BKf": ("sbuf", [128, 128], "float32"), "BKn": ("sbuf", [128, 128], "bfloat16"), "BK8": ("sbuf", [128, 128], "bfloat16"),
    "L0": ("sbuf", [128, 128], "float32"), "L15": ("sbuf", [128, 128], "float32"), "LD": ("sbuf", [128, 128], "float32"),
    "RS": ("sbuf", [128, 256], "float32"), "RN": ("sbuf", [128, 128], "bfloat16"), "RB": ("sbuf", [128, 128], "bfloat16"),
    "NB": ("sbuf", [128, 128], "bfloat16"), "J4": ("sbuf", [128, 128], "bfloat16"), "Z": ("sbuf", [128, 512], "bfloat16"), "c15": ("sbuf", [128, 8], "bfloat16"),
    "cb": ("sbuf", [128, 1], "float32"), "cy": ("sbuf", [128, 1], "float32"), "Hb": ("sbuf", [128, 128], "bfloat16"), "HH": ("sbuf", [128, 128], "bfloat16"),
    "b0": ("psum", [128, 512], "float32"), "b1": ("psum", [128, 512], "float32"), "b2": ("psum", [128, 512], "float32"), "b3": ("psum", [128, 512], "float32"),
    "b4": ("psum", [128, 512], "float32"), "b5": ("psum", [128, 512], "float32"), "b6": ("psum", [128, 512], "float32"), "b7": ("psum", [128, 512], "float32"),
}
SMALL = {}
for _b, _l in (("LI", "q r sg a s2 a1 dl fs f k o1 o2 CL C16 Ai Am"), ("LF", "lt nk pr prb fx fx2 fm fm2 fo fo2 uy uz ow CW CK CU CF CF2 cnt Af thr")):
    for _i, _n in enumerate(_l.split()):
        SMALL[_n] = (_b, 16 * _i, 16 * _i + (1 if _n in ("Ai", "Am", "cnt", "Af", "thr") else 16))
for _n, _a, _z in (("fk", "f", "k"), ("pp", "pr", "prb"), ("fxx", "fx", "fx2"), ("fmm", "fm", "fm2"), ("foo", "fo", "fo2"), ("CWK", "CW", "CK"), ("CFF", "CF", "CF2")):
    SMALL[_n] = (SMALL[_a][0], SMALL[_a][1], SMALL[_z][2])
for _n in ("K", "P"):
    for _t in range(R):
        SCRATCH["%sl%d" % (_n, _t)] = ("sbuf", [128, 256], "uint16")
        if _t < R - 1:
            SCRATCH["%so%d" % (_n, _t)] = ("sbuf", [128, 256], "uint16")

SEMAPHORES = ["v", "s", "t", "p", "ls", "dx", "dk", "dp", "dw", "dw2", "dkd", "df", "dy1", "dy2", "dy3"] + ["%sa%d" % (n, t) for n in "KP" for t in range(1, R)]


def rank_program(g, core, T, topo):
    rank = T.rank_of(core)
    if rank is None:
        return
    nxt, prv = T.cores[(rank + 1) % 4], T.cores[(rank + 3) % 4]
    queues = {"v": g.vector, "s": g.scalar, "t": g.tensor, "p": g, "y": g.sync}
    cnt = {}
    known = {q: {} for q in queues}
    snaps = {}
    recs = {}

    def bank(b):
        return len(b) == 2 and b[0] == "b" and b[1].isdigit()

    def key(x):
        return x if isinstance(x, tuple) else (x, 0, 1 << 30)

    def sync(q, reads, writes):
        need = {}
        for accs, wr in ((reads, False), (writes, True)):
            for x in accs:
                b, lo, hi = key(x)
                for (l2, h2, q2, sm, val, w2) in recs.get(b, ()):
                    if bank(b):
                        hit = q2 != q or (q != "t" and (wr or w2) and l2 < hi and lo < h2)
                    else:
                        hit = (wr or w2) and l2 < hi and lo < h2 and not q2 == q == "t"
                    if hit and val > known[q].get(sm, 0):
                        need[sm] = max(need.get(sm, 0), val)
        kn = known[q]
        for sm in sorted(need):
            if any(o != sm and snaps.get((o, need[o]), {}).get(sm, 0) >= need[sm] for o in need):
                continue
            queues[q].wait_ge(T.sem[sm], need[sm])
        for sm, val in need.items():
            for o, x in snaps.get((sm, val), {}).items():
                kn[o] = max(kn.get(o, 0), x)
            kn[sm] = max(kn.get(sm, 0), val)

    def note(q, reads, writes, sm, val):
        snap = dict(known[q])
        snap[sm] = max(snap.get(sm, 0), val)
        snaps[(sm, val)] = snap
        for accs, wr in ((reads, False), (writes, True)):
            for x in accs:
                b, lo, hi = key(x)
                old = recs.get(b, [])
                if wr and not bank(b):
                    old = [e for e in old if not (lo <= e[0] and e[1] <= hi)]
                old = [e for e in old if not (e[2] == q and e[3] == sm and e[0] >= lo and e[1] <= hi and (wr or not e[5]))]
                recs[b] = old + [(lo, hi, q, sm, val, wr)]

    def op(q, call, reads, writes):
        sync(q, reads, writes)
        cnt[q] = cnt.get(q, 0) + 1
        call().then_inc(T.sem[q], 1)
        note(q, reads, writes, q, cnt[q])

    def dmas(q, sm, pairs, reads, writes):
        sync(q, reads, writes)
        for out, in_ in pairs:
            queues[q].dma_start(out, in_).then_inc(T.sem[sm], 16)
            cnt[sm] = cnt.get(sm, 0) + 16
        note(q, reads, writes, sm, cnt[sm])

    V, S, E = g.vector, g.scalar, g.tensor

    def pa(x):
        return x[3] if len(x) > 3 else T[x[0]][:, x[1]:x[2]]

    def ks(*xs):
        return [x[:3] for x in xs if isinstance(x, tuple)] + [x[4] for x in xs if isinstance(x, tuple) and len(x) > 4]

    def v_tt(o, a, b, f):
        op("v", lambda: V.tensor_tensor(pa(o), pa(a), pa(b), f), ks(a, b), ks(o))

    def v_ts(o, a, x, f, y=None, f2=None):
        x1 = pa(x) if isinstance(x, tuple) else x
        if f2 is None:
            op("v", lambda: V.tensor_scalar(pa(o), pa(a), x1, None, f), ks(a, x), ks(o))
        else:
            op("v", lambda: V.tensor_scalar(pa(o), pa(a), x1, y, f, f2), ks(a, x), ks(o))

    def v_cp(o, a):
        op("v", lambda: V.tensor_copy(pa(o), pa(a)), ks(a), ks(o))

    def v_scan(o, d0, d1, init, f, f2):
        op("v", lambda: V.tensor_tensor_scan(pa(o), pa(d0), pa(d1), init, f, f2), ks(d0, d1), ks(o))

    def v_ms(o, c):
        op("v", lambda: V.memset(pa(o), c), [], ks(o))

    def s_act(o, a, f):
        op("s", lambda: S.activation(pa(o), pa(a), f), ks(a), ks(o))

    def s_mul(o, a, c):
        op("s", lambda: S.activation(pa(o), pa(a), F.Copy, scale=c), ks(a), ks(o))

    def mm(o, l, r, start, stop):
        op("t", lambda: E.matmul(pa(o), pa(l), pa(r), start, stop), ks(l, r), ks(o))

    def iota(o, pattern, base, cm):
        flag = {} if o[0] in ("ia", "ib", "ic", "idd", "LI") else {"allow_small_or_imprecise_dtypes": True}
        op("p", lambda: g.iota(pa(o), pattern, base, cm, **flag), [], ks(o))

    def ind(w, lo, hi, u, c0, c1):
        return (w, lo, hi, T[w][:, lo:hi].indirect(T[u][:, c0:c1]), (u, c0, c1))

    def st(b, lo, hi, step):
        return (b, lo, hi, T[b][:, lo:hi:step])

    def rev(b, lo, hi):
        return (b, lo, hi, T[b][:, hi - 1:lo - 1:-1] if lo else T[b][:, hi - 1::-1])

    def full(b):
        return SMALL[b] if b in SMALL else (b, 0, int(SCRATCH[b][1][-1]))

    def h8(b, h):
        x = full(b)
        return (x[0], x[1] + h * 8, x[1] + h * 8 + 8)

    def half(b, h):
        return (b, h * H, h * H + H)

    for t in range(1, R):
        for n, src in (("K", prv), ("P", nxt)):
            sm = "%sa%d" % (n, t)
            cnt[sm] = len(topo.engines(src, core))
            recs["%sl%d" % (n, t)] = [(0, 256, "r", sm, cnt[sm], True)]
    dmas("y", "dp", [(T.PI[:], T.ph[:])], [], ["PI"])
    dmas("y", "dk", [(T.KI[:], T.ka[:])], [], ["KI"])
    dmas("y", "dx", [(T.X[:, 0:4096], T.x0[:])], [], [("X", 0, 4096)])

    iota(full("ia"), [[1, 256]], 256, -1)
    iota(full("ib"), [[0, 256]], 0, 1)
    iota(full("ic"), [[1, 256]], 0, 0)
    iota(full("J4"), [[0, 8], [4096, 16]], 0, 0)
    iota(full("CL"), [[16, 16]], 0, 0)
    iota(("W", 0, 17 * 256), [[0, 17 * 256]], 0, 0)
    iota(("W", 17 * 256, WW), [[1, 256]], 4096, 0)
    iota(full("FF"), [[0, FW]], 0, 0)
    v_ms(("X", 4096, XW), 0.0)
    v_ms(full("Z"), 0.0)
    v_ms(full("NB"), -864.0 * 65536)
    v_ms(full("c15"), 15.0)
    v_ms(("FD", 0, 1), 0.0)
    v_ms(full("Af"), 0.0)
    v_ms(full("thr"), 160.0 * 65536 - 1)
    v_ms(full("KD"), 0.0)
    v_ms(full("CF"), 16.0)
    v_ms(full("CF2"), 17.0)
    v_ms(full("cb"), -2000.5)
    v_ms(full("cy"), -127.5)
    v_ms(full("HH"), 0.5)
    v_cp(full("Pl0"), full("PI"))
    v_cp(full("Kl0"), full("KI"))
    dmas("y", "dkd", [(T.kd[:, 0:1, :], T.KD[0:8, 0:256])], ["KD"], ["kd0"])
    v_ts(full("If"), ("ia", 0, 128), 256.0, A.is_equal)
    s_act(full("Ib"), full("If"), F.Copy)
    s_mul(full("In"), full("If"), -1.0)
    s_mul(full("Hb"), full("If"), 0.5)
    v_ts(full("idd"), full("ia"), 15, A.bitwise_and)
    v_ts(full("mf"), ("idd", 0, 128), 0.0, A.is_equal)
    s_act(full("mb"), full("mf"), F.Copy)
    v_ts(full("OD"), full("idd"), 0.0, A.not_equal, OFF, A.mult)
    v_ts(full("ia"), full("ib"), 4, A.arith_shift_right)
    v_tt(full("B8f"), ("ia", 0, 8), ("ic", 0, 8), A.is_equal)
    s_act(full("B8"), full("B8f"), F.Copy)
    s_mul(full("WN"), full("B8f"), -65536.0)
    s_mul(full("WP"), full("B8f"), 65536.0)
    s_mul(full("WR"), full("B8f"), 131072.0)
    s_mul(full("B8n"), full("B8f"), -1.0)
    s_mul(full("B82"), full("B8f"), 2.0)
    v_ts(full("idd"), full("ic"), 4, A.arith_shift_right)
    v_tt(full("BKf"), ("ia", 0, 128), ("idd", 0, 128), A.is_equal)
    s_mul(full("BK8"), full("BKf"), 8192.0)
    v_ts(full("ic"), full("ic"), 15, A.bitwise_and)
    v_ts(full("ib"), full("ib"), 15, A.bitwise_and)
    v_ts(full("RS"), full("ic"), 0.0, A.is_equal, BIG, A.mult)
    v_ts(full("RB"), ("ic", 0, 128), 0.0, A.is_equal, 1024.0, A.mult)
    v_ts(full("RN"), full("RB"), -1.0, A.add)
    v_ts(full("L0"), ("ic", 0, 128), 4.0 * NB1, A.is_ge, -1.0, A.mult)
    v_tt(full("BKn"), full("L0"), full("BKf"), A.mult)
    v_ts(full("L0"), ("ib", 0, 128), 0.0, A.is_equal)
    v_tt(full("L0"), full("L0"), full("BKf"), A.mult)
    v_ts(full("L15"), ("ib", 0, 128), 15.0, A.is_equal)
    v_tt(full("L15"), full("L15"), full("BKf"), A.mult)
    v_tt(full("LD"), full("If"), full("L15"), A.subtract)
    v_ts(full("If"), ("ic", 0, 128), 0.0, A.not_equal)
    v_tt(full("L15"), full("L15"), full("If"), A.mult)
    v_tt(full("CL"), full("CL"), ("ib", 0, 16), A.add)
    v_ts(full("C16"), full("CL"), 16.0, A.mult)
    v_ts(h8("C16", 1), h8("C16", 1), -2048.0, A.add)
    v_ts(full("CW"), full("CL"), 4096.0, A.add)
    v_ts(full("CK"), full("CL"), 17 * 256.0, A.add)
    v_ts(full("CU"), full("CL"), 256.0, A.add)

    hb = ("b0", "b1")
    KEY = [(hb[h], 0, 128) for h in range(2)]
    ND = [(hb[h], 128, 256) for h in range(2)]
    QT = [(hb[h], 264, 272) for h in range(2)]
    KILL = [("b2", 0, 128), ("b2", 128, 256)]
    XP = ("b2", 256, 384)
    QL = [("b2", 384, 392), ("b2", 392, 400)]
    VP, VE, ME = ("b3", 0, 256), ("b4", 0, 256), ("b5", 0, 256)
    NEAR = ("b4", "b5", "b6", "b7")

    def strip(k, j):
        return (k[0], k[1], k[2], T[k[0]][:, k[1] + j:k[2]:16])

    def group(k, src, w, stop=False, step=16, js=range(LO)):
        for j in js:
            x = st(src, j, 2048, 16) if step == 16 else (src, j * 128, j * 128 + 128)
            mm(strip(k, j), x, full(w), False, stop and j == js[-1])

    def bias(h):
        mm(KEY[h], full("Ib"), full("NB"), True, False)
        mm(KEY[h], full("Ib"), full("J4"), False, False)

    def best(h):
        v_scan(half("KM", h), ("RS", 0, 128), KEY[h], BIG, A.add, A.min)
        v_scan(rev("KC", h * H, h * H + H), ("RS", 0, 128), rev("KM", h * H, h * H + H), BIG, A.add, A.min)
        v_tt(half("QM", h), half("KC", h), full("mf"), A.mult)
        op("s", lambda: S.activation(pa(half("KB", h)), pa(half("KC", h)), F.Sign, bias=T.cb[:], scale=-1.0), [half("KC", h), full("cb")], [half("KB", h)])

    def best_t(h):
        mm(QL[h], half("QM", h), full("B8f"), True, True)
        mm(KILL[h], half("KB", h), full("Hb"), True, False)
        mm(KILL[h], full("Ib"), full("HH"), False, True)

    def pick(h):
        q, r, sg, a, s2, a1, dl, fs, f, o1 = [h8(n, h) for n in ("q", "r", "sg", "a", "s2", "a1", "dl", "fs", "f", "o1")]
        v_ts(q, QL[h], 2047.0, A.add)
        v_ts(sg, q, 11, A.arith_shift_right, 1, A.bitwise_and)
        v_ts(a, q, 16, A.arith_shift_right, 3, A.bitwise_and)
        v_ts(s2, sg, 2.0, A.mult, -1.0, A.add)
        v_ts(a1, a, 1.0, A.add)
        v_ts(r, q, 12, A.arith_shift_right)
        v_tt(dl, s2, a1, A.mult)
        v_tt(fs, r, dl, A.add)
        v_ts(f, fs, 15, A.bitwise_and)
        v_tt(o1, f, h8("C16", h), A.add)
        v_cp(full("uf%d" % h), o1)

    def near_open(b):
        mm((NEAR[b], 0, 512), full("Ib"), full("Z"), True, False)

    def near_load(b, srcs):
        for i, src in enumerate(srcs):
            for j in range(4):
                mm((NEAR[b], j * 128, j * 128 + 128), full("Ib"), st(src, 4 * b + j, 2048, 16), False, False)

    def near_diff(b, xn, out):
        for j in range(4):
            mm((NEAR[b], j * 128, j * 128 + 128), full("In"), full(xn), False, j == 3)
        s_act((out, b * 512, b * 512 + 512), (NEAR[b], 0, 512), F.Abs)

    def penalty(h):
        v_ts(half("pen", h), ND[h], 1024.0, A.is_ge, 16.0, A.mult)
        v_scan(half("ts", h), full("RN"), half("pen", h), 1024.0, A.add, A.min)
        v_scan(rev("tb", h * H, h * H + H), full("RB"), rev("ts", h * H, h * H + H), 1024.0, A.add, A.min)
        v_tt(half("tm", h), half("tb", h), full("mb"), A.mult)
        mm(QT[h], full("Ib"), full("c15"), True, False)
        mm(QT[h], half("tm", h), full("B8"), False, True)

    def send(n, t, dst):
        b, l, sm = "%so%d" % (n, t), "%sl%d" % (n, t + 1), "%sa%d" % (n, t + 1)
        rid, pid, _ = topo.addr(dst)
        sync("p", [full(b)], [])
        g.remote_dma(T[l][:], T[b][:], T.sem[sm], T.sem.ls, pid, rid, topo.mask(core, dst))
        cnt["ls"] = cnt.get("ls", 0) + len(topo.engines(core, dst))

    def thresh(t):
        if t:
            v_tt(full("Af"), full("Af"), full("cnt"), A.add)
            v_cp(full("Ai"), full("Af"))
            v_ts(full("Am"), full("Ai"), 15, A.bitwise_and)
            v_ts(full("thr"), full("Am"), 262144.0, A.mult, 160.0 * 65536 - 1, A.add)

    FK = ["F%d" % j for j in range(1, 15)] + ["F17"]
    recs.update({k: list(recs["FF"]) for k in FK})
    recs.update({"W0": list(recs["W"]), "W16": list(recs["W"])})
    WK = ["W0", "W16", "W"]

    for t in range(R):
        Kl, Pl = "Kl%d" % t, "Pl%d" % t
        last = t == R - 1

        def own_names():
            mm(VP, full("L0"), full("VG"), True, True)

        def own_marks():
            for x in (VE, ME):
                mm(x, full("L0"), full("VG"), True, False)
                mm(x, full("Ib"), full("OD"), False, x is VE)

        def near_max():
            for j in range(4 * NB1, LO):
                v_tt(("M1", j * 128, j * 128 + 128), st("S1", j, 2048, 16), XP, A.max)
                mm(strip(ND[1], j), ("M1", j * 128, j * 128 + 128), full("B82"), False, j == LO - 1)

        def write_table():
            v_scan(full("RU"), full("RS"), VE, BIG, A.add, A.min)
            v_cp(full("Vu"), VP)
            v_tt(("FD", 1, 256), ("b3", 1, 256), ("RU", 0, 255), A.is_equal)
            mm(ME, full("BK8"), full("FD"), False, False)
            for c in range(15):
                lo = 16 * c + 16
                v_ts(("EQ", c * 256 + lo, c * 256 + 256), ("Vu", lo, 256), ("RU", 16 * c + 15, 16 * c + 16), A.is_equal)
                mm(("b5", lo, 256), full("BK8"), ("EQ", c * 256 + lo, c * 256 + 256), False, c == 14)
            s_act(("YK", 0, 128), ind("Y0", 0, 2048, "uk", 0, 8), F.Copy)
            s_act(("AD", 0, 128), ind("D0", 0, 2048, "uk", 0, 8), F.Abs)
            s_act(full("SK1"), ind("S1", 0, 2048, "uk", 8, 16), F.Copy)
            s_act(("AD", 128, 256), ind("D1", 0, 2048, "uk", 8, 16), F.Abs)
            op("s", lambda: S.activation(T.KJ[:], T.b2[:, 0:256], F.Copy, accum_out=pa(full("cnt"))), [("b2", 0, 256)], [full("KJ"), full("cnt")])
            v_tt(("YK", 128, 256), ind("D1", 0, 2048, "uk", 8, 16), full("SK1"), A.add)
            v_ts(full("w2"), full("AD"), 32.0, A.is_le, -128.0, A.mult)
            op("s", lambda: S.activation(T.b6[:, 0:256], T.YK[:], F.Sign, bias=T.cy[:]), [full("YK"), full("cy")], [("b6", 0, 256)])
            v_tt(full("wg"), full("w2"), ("b6", 0, 256), A.mult)
            v_scan(full("SE"), full("RS"), ME, BIG, A.add, A.min)
            v_tt(full("ow"), st("SE", 15, 256, 16), full("CW"), A.min)
            v_cp(full("uX"), full("ow"))
            xs = T.X[:, 0:XW].indirect(T.uX[:, 0:16])
            op("v", lambda: V.tensor_tensor(xs, T.YK[:], T.wg[:], A.add), [full("uX"), full("YK"), full("wg")], ["X"])

        v_cp(full("PF"), full("PI") if t == 0 else full(Pl))
        dmas("y", "dw", [(T.W[0::16, 0:4096], T.PF[:])], ["PF"], ["W0"])
        n, l = 2048 // CH, 128 // CH
        for c in range(CH):
            s_act(("Y0", c * n, c * n + n), ind("X", 0, 4096, Pl, c * l, c * l + l), F.Copy)
        v_cp(full("KF"), full("KI") if t == 0 else full(Kl))
        bias(0)
        mm(("b3", 0, 256), full("LD"), full("KF"), True, True)
        bias(1)
        mm(("b3", 256, 512), full("L15"), full("KF"), True, True)
        for b in range(4):
            near_open(b)
        for c in range(CH):
            v_tt(("D0", c * n, c * n + n), ind("X", 0, 4096, Kl, c * l, c * l + l), ("Y0", c * n, c * n + n), A.subtract)
        s_act(full("KD"), ("b3", 0, 256), F.Copy)
        for c in range(2):
            s_act(("S1", c * 1024, c * 1024 + 1024), ind("X", 0, 4096, Kl, 128 + c * 64, 192 + c * 64), F.Copy)
        s_act(full("K15"), ("b3", 256, 512), F.Copy)
        dmas("y", "dkd", [(T.kd[:, 1:17, :], T.KD[:])], ["KD"], ["kd"])
        dmas("y", "dw2", [(T.W[0::16, 4096:4352], T.KF[0::16, :])], ["KF"], ["W16"])
        dmas("y", "df", [(T.FF[j::16, 256:(16 - j) * 256], T.kd[:, j + 1:16, :]) for j in range(1, 15)] + [(T.FF[:, 17 * 256:18 * 256], T.kd[:, 0:16, :])], ["kd", "kd0"], FK)
        group(KEY[0], "D0", "WN")
        v_ts(full("R0"), full("D0"), 0.0, A.max)
        group(KEY[0], "R0", "WR")
        group(KEY[0], "D0", "B8", stop=True)
        for c in range(2):
            v_tt(("D1", c * 1024, c * 1024 + 1024), ind("X", 0, 4096, Pl, 128 + c * 64, 192 + c * 64), ("S1", c * 1024, c * 1024 + 1024), A.subtract)
        for c in range(2):
            s_act(("R1", c * 1024, c * 1024 + 1024), ("D1", c * 1024, c * 1024 + 1024), F.Abs)
        near_load(0, ("D0", "Y0"))
        near_load(1, ("D0", "Y0"))
        best(0)
        best_t(0)
        v_tt(full("kp"), full("KF"), full("PF"), A.mult)
        group(KEY[1], "R1", "WP")
        group(KEY[1], "D1", "B8n", stop=True)
        pick(0)
        s_act(full("XN0"), ind("Y0", 0, 2048, "uf0", 0, 8), F.Copy)
        best(1)
        near_diff(0, "XN0", "A0")
        best_t(1)
        v_ts(full("kq"), full("kp"), 5, A.arith_shift_right)
        thresh(t)
        pick(1)
        near_diff(1, "XN0", "A0")
        s_act(full("SF1"), ind("S1", 0, 2048, "uf1", 0, 8), F.Copy)
        for b in range(2, 4):
            near_load(b, ("D0", "Y0"))
            near_diff(b, "XN0", "A0")
        v_tt(full("p1"), full("kq"), ("b2", 0, 256), A.mult)
        v_tt(full("XN1"), ind("D1", 0, 2048, "uf1", 0, 8), full("SF1"), A.add)
        mm(XP, full("Ib"), full("XN1"), True, True)
        mm(ND[1], full("XN1"), full("BKn"), True, False)
        for b in range(NB1):
            near_open(b)
            near_load(b, ("S1",))
            near_diff(b, "XN1", "A1")
        group(ND[1], "S1", "B8n", js=range(4 * NB1, LO))
        mm(ND[0], full("Ib"), ("Z", 0, 128), True, False)
        v_tt(full("p2"), full("p1"), full("PF"), A.add)
        v_ts(full("p3"), full("p2"), 4095, A.bitwise_and)
        if not last:
            v_cp(full("Po%d" % t), full("p3"))
            send("P", t, prv)
        v_ts(full("nk"), full("q"), 47.0, A.is_ge)
        v_ts(full("lt"), full("q"), full("thr"), A.is_lt, 256.0, A.mult)
        v_ts(full("k"), full("r"), 15, A.bitwise_and)
        v_tt(full("pr"), full("nk"), full("lt"), A.mult)
        v_tt(full("prb"), full("nk"), full("lt"), A.mult)
        v_tt(full("fxx"), full("fk"), full("CFF"), A.subtract)
        v_tt(full("o2"), full("k"), full("C16"), A.add)
        v_tt(full("fmm"), full("fxx"), full("pp"), A.mult)
        v_cp(full("uk"), full("o2"))
        v_tt(full("foo"), full("fmm"), full("CWK"), A.add)
        v_cp(full("uWV"), full("foo"))
        vw = ind("W", 0, WW, "uWV", 16, 32)
        op("s", lambda: S.activation(T.VG[:], vw[3], F.Copy), WK + [full("uWV")], ["VG"])
        if last:
            own_names()
            own_marks()
        group(ND[0], "A0", "B8", stop=True, step=1)
        group(ND[1], "A1", "B8", step=1, js=range(4 * NB1))
        near_max()
        if last:
            write_table()
            dmas("y", "dy3", [(T.yx[:], T.X[:, 0:4096])], ["X"], ["yx"])
        penalty(0)
        if not last:
            own_names()
        bw = ind("W", 0, WW, "uWV", 0, 16)
        op("v", lambda: V.tensor_tensor(T.BA[:], bw[3], T.K15[:], A.add), WK + [full("uWV"), full("K15")], ["BA"])
        penalty(1)
        if not last:
            own_marks()
        for h in range(2):
            v_tt(h8("uy", h), QT[h], h8("pr", h), A.mult)
            v_tt(h8("uz", h), h8("uy", h), h8("CU", h), A.add)
        v_cp(full("uu"), full("uz"))
        fw = ind("FF", 0, FW, "uu", 0, 16)
        op("v", lambda: V.tensor_tensor(T.KN[:], fw[3], T.BA[:], A.add), FK + ["FF", full("uu"), full("BA")], [full("KN")])
        if not last:
            v_cp(full("Ko%d" % t), full("KN"))
            send("K", t, nxt)
            write_table()
        else:
            dmas("y", "dy1", [(T.yk[:], T.KN[:])], ["KN"], ["yk"])
            v_cp(full("PF"), full("p3"))
            dmas("y", "dy2", [(T.yp[:], T.PF[:])], ["PF"], ["yp"])
    for sm, val in sorted(cnt.items()):
        g.wait_ge(T.sem[sm], val)
